import numpy as np
import ml_dtypes


def mxq(x, axis, fmt="e4m3"):
    dtype, down = {"e4m3": (ml_dtypes.float8_e4m3fn, 7), "e5m2": (ml_dtypes.float8_e5m2, 14)}[fmt]
    v = np.moveaxis(np.asarray(x, np.float32).astype(ml_dtypes.bfloat16).astype(np.float64), axis, -1)
    blocks = v.reshape(v.shape[:-1] + (-1, 32))
    amax = np.abs(blocks).max(-1, keepdims=True)
    byte = np.maximum(np.where(amax > 0, np.frexp(amax)[1] - 1 + 127, 0) - down, 1)
    scale = np.exp2(byte - 127.0)
    codes = (blocks / scale).astype(np.float32).astype(dtype).astype(np.float64)
    return np.moveaxis((codes * scale).reshape(v.shape), -1, axis)


WIDE = False


def mx_kscale(k):
    if not WIDE:
        return np.ones(k)
    levels = np.array([10, -10, 5, -5, 0])
    if k % 512:
        return np.exp2(np.random.permutation(np.resize(levels, k // 32))).repeat(32)
    a = np.empty((k // 512, 16))
    for p in range(k // 512):
        a[p, :8] = np.random.permutation(np.resize(levels, 8))
        for g in range(8):
            far = levels[np.abs(levels - a[p, g]) >= 10]
            a[p, g + 8] = far[np.random.randint(len(far))]
    return np.exp2(a.ravel()).repeat(32)


def f64(x):
    return np.asarray(x).astype(np.float64)


def striped(idx):
    return np.tile(idx.reshape(-1, 16).T, (8, 1)).astype(np.uint16)


def unstriped(offs):
    return offs[:16].T.reshape(-1).astype(np.int64)


def pack_weight(w):
    k, n = w.shape
    w = f64(np.asarray(w, np.float32).astype(ml_dtypes.bfloat16)).reshape(k // 32, 32, n)
    amax = np.abs(w).max(1)
    byte = np.clip(np.where(amax > 0, np.frexp(amax)[1] - 1 + 127 - 7, 1), 1, 254)
    scaled = (w * np.exp2(127.0 - byte)[:, None, :]).reshape(k, n).astype(np.float32)
    words = np.ascontiguousarray(scaled.reshape(k // 512, 128, 4, n).transpose(0, 1, 3, 2)).astype(ml_dtypes.float8_e4m3fn).view(np.uint8)
    return words, np.ascontiguousarray(byte.astype(np.uint8).reshape(k // 512, 16, n))


def unpack_weight(words, scales):
    g, p, n, _ = words.shape
    vals = np.ascontiguousarray(words).view(ml_dtypes.float8_e4m3fn).astype(np.float64) * np.repeat(np.exp2(scales.astype(np.float64) - 127.0), 8, axis=1)[..., None]
    return vals.transpose(0, 1, 3, 2).reshape(g * 512, n)


K, T, S, N, R = 512, 1024, 512, 128, 256


def setup_inputs():
    n = np.random.standard_normal
    s = mx_kscale(K)[:, None]
    packed_xT = pack_weight(n((K, T)) * s)
    return {
        "x_words": packed_xT[0],
        "x_scales": packed_xT[1],
        "w1": (n((K, N)) / np.sqrt(K) / s).astype(np.float32),
        "slo": (np.random.uniform(0.5, 2.0, (N, R))).astype(np.float32),
        "icp": (n((N, R))).astype(np.float32),
        "lob": (-np.random.uniform(0.5, 1.5, (N, R))).astype(np.float32),
        "true": (n((N, S))).astype(np.float32),
        "offs": striped(np.random.permutation(T)[:S]),
        "seg": striped(np.random.permutation(np.concatenate([np.arange(R), np.random.randint(0, R, S - R)]))),
    }


def reference(x_words, x_scales, w1, slo, icp, lob, true, offs, seg):
    slog = f64(slo)[:, unstriped(seg)]
    xq = unpack_weight(x_words, x_scales)[:, unstriped(offs)]
    y = mxq(f64(w1), 0, "e4m3").T @ xq
    icpg = f64(icp)[:, unstriped(seg)]
    pos = slog * y + icpg
    lobg = f64(lob)[:, unstriped(seg)]
    pcl = np.maximum(pos, lobg)
    return (f64(true) - pcl) ** 2 - (0.5 * ((f64(true) - (np.maximum(np.pad(pcl, ((0, 0), (1, 0)))[:, :S], pcl))) ** 2))

@@ -1,0 +1,116 @@
+from contextlib import ExitStack
+
+import concourse.mybir as mybir
+
+K, T, S, N, R = 512, 1024, 512, 128, 256
+FLOPS = 2 * K * N * S
+
+F32 = mybir.dt.float32
+BF16 = mybir.dt.bfloat16
+I32 = mybir.dt.int32
+U32 = mybir.dt.uint32
+U16 = mybir.dt.uint16
+U8 = mybir.dt.uint8
+FP8X4 = mybir.dt.float8_e4m3fn_x4
+ALU = mybir.AluOpType
+ACT = mybir.ActivationFunctionType
+
+P = 128
+PACK = 4
+HALF = S // 2
+SPARE = 16
+LEAD = 4
+
+
+def tile_picked_yrmidx_mono_p_kernel(tc, x_words, x_scales, w1, slo, icp, lob, true, offs, seg, out):
+    nc = tc.nc
+    with ExitStack() as ctx:
+        lists = ctx.enter_context(tc.tile_pool(name="lists", bufs=1))
+        sb = ctx.enter_context(tc.tile_pool(name="sb", bufs=1))
+        psum = ctx.enter_context(tc.psum_pool(name="psum", bufs=1))
+
+        offs_t = lists.tile([P, S // 16], U16, name="offs_t")
+        seg_t = lists.tile([P, S // 16], U16, name="seg_t")
+        words = sb.tile([P, T], I32, name="words", align_bytes=64)
+        scales = sb.tile([P, T], U8, name="scales", align_bytes=64)
+        w_raw = sb.tile([P, PACK, N], F32, name="w_raw", align_bytes=64)
+        slo_t = sb.tile([P, R + SPARE], F32, name="slo_t", align_bytes=64)
+        icp_t = sb.tile([P, R + SPARE], F32, name="icp_t", align_bytes=64)
+        lob_t = sb.tile([P, R + SPARE], F32, name="lob_t", align_bytes=64)
+        true_t = sb.tile([P, S], F32, name="true_t", align_bytes=64)
+        pcl = sb.tile([P, LEAD + S], F32, name="pcl", align_bytes=64)
+
+        nc.vector.memset(lob_t[:, R:], 0.0)
+        nc.vector.memset(slo_t[:, R:], 0.0)
+        nc.vector.memset(icp_t[:, R:], 0.0)
+        nc.vector.memset(pcl[:, 0:LEAD], 0.0)
+
+        nc.sync.dma_start(offs_t[:], offs)
+        rows = x_scales[0].bitcast(I32)
+        for q in range(4):
+            queue = nc.sync if q < 2 else nc.scalar
+            queue.dma_start(scales[32 * q : 32 * (q + 1), :].bitcast(I32), rows[4 * q : 4 * q + 4, :].unsqueeze(0).broadcast_to([8, 4, T // 4]))
+        nc.sync.dma_start(words[:], x_words[0].rearrange("p c t -> p (c t)").bitcast(I32))
+        nc.sync.dma_start(w_raw[:], w1.rearrange("(p t) n -> p t n", t=PACK))
+        nc.sync.dma_start(seg_t[:], seg)
+        nc.sync.dma_start(lob_t[:, 0:R], lob)
+        nc.sync.dma_start(slo_t[:, 0:R], slo)
+        nc.sync.dma_start(icp_t[:, 0:R], icp)
+        nc.sync.dma_start(true_t[:], true)
+
+        w_bf = sb.tile([P, N, PACK], BF16, name="w_bf", align_bytes=64)
+        nc.scalar.activation(w_bf[:], w_raw[:].rearrange("p t n -> p n t"), ACT.Copy)
+        w_codes = sb.tile([P, N], U32, name="w_codes", align_bytes=64)
+        w_scales = sb.tile([P, N], U8, name="w_scales", align_bytes=64)
+
+        halves = [slice(h * HALF, (h + 1) * HALF) for h in range(2)]
+        cols16 = [slice(h * HALF // 16, (h + 1) * HALF // 16) for h in range(2)]
+
+        def tiles(name, dtype):
+            return [sb.tile([P, HALF], dtype, name=f"{name}{h}", align_bytes=64) for h in range(2)]
+
+        lobg = tiles("lobg", F32)
+        x_codes = tiles("x_codes", U32)
+        x_bytes = tiles("x_bytes", U8)
+        y = tiles("y", F32)
+        prod = tiles("prod", F32)
+        pos = tiles("pos", F32)
+        runmax = tiles("runmax", F32)
+        err1 = tiles("err1", F32)
+        err2 = tiles("err2", F32)
+        sq1 = tiles("sq1", F32)
+        sq2 = tiles("sq2", F32)
+        res = tiles("res", F32)
+        acc = [psum.tile([P, HALF], F32, name=f"acc{h}") for h in range(2)]
+
+        def product(h):
+            nc.tensor.matmul_mx(out=acc[h][:], lhsT=w_codes[:].bitcast(FP8X4), lhsT_scale=w_scales[:],
+                                rhs=x_codes[h][:].bitcast(FP8X4), rhs_scale=x_bytes[h][:], start=True, stop=True)
+            nc.scalar.copy(y[h][:], acc[h][:])
+
+        for h in range(2):
+            nc.vector.tensor_copy(x_bytes[h][:], scales[:].indirect(offs_t[:, cols16[h]]))
+        for h in range(2):
+            nc.vector.tensor_copy(x_codes[h][:], words[:].bitcast(U32).indirect(offs_t[:, cols16[h]]))
+        nc.vector.quantize_mx(out=w_codes[:].bitcast(FP8X4), scales=w_scales[:], in_=w_bf[:].rearrange("p n t -> p (n t)"))
+        for h in range(2):
+            product(h)
+        for h in range(2):
+            nc.vector.tensor_copy(lobg[h][:], lob_t[:].indirect(seg_t[:, cols16[h]]))
+        for h in range(2):
+            nc.vector.tensor_tensor(prod[h][:], slo_t[:].indirect(seg_t[:, cols16[h]]), y[h][:], ALU.mult)
+        for h in range(2):
+            nc.vector.tensor_tensor(pos[h][:], icp_t[:].indirect(seg_t[:, cols16[h]]), prod[h][:], ALU.add)
+        here = [slice(LEAD + h * HALF, LEAD + (h + 1) * HALF) for h in range(2)]
+        before = [slice(LEAD - 1 + h * HALF, LEAD - 1 + (h + 1) * HALF) for h in range(2)]
+        for h in range(2):
+            nc.vector.tensor_tensor(pcl[:, here[h]], pos[h][:], lobg[h][:], ALU.max)
+        for h in range(2):
+            nc.vector.tensor_tensor(runmax[h][:], pcl[:, before[h]], pcl[:, here[h]], ALU.max)
+            nc.vector.tensor_tensor(err1[h][:], true_t[:, halves[h]], pcl[:, here[h]], ALU.subtract)
+            nc.scalar.activation(sq1[h][:], err1[h][:], ACT.Square)
+            nc.vector.tensor_tensor(err2[h][:], true_t[:, halves[h]], runmax[h][:], ALU.subtract)
+            nc.scalar.activation(sq2[h][:], err2[h][:], ACT.Square)
+        for h in range(2):
+            nc.vector.scalar_tensor_tensor(res[h][:], sq2[h][:], -0.5, sq1[h][:], ALU.mult, ALU.add)
+            nc.sync.dma_start(out[:, halves[h]], res[h][:])

@@ -33,7 +33,7 @@ def tile_picked_yrmidx_mono_p_kernel(tc, x_words, x_scales, w1, slo, icp, lob, t
         seg_t = lists.tile([P, S // 16], U16, name="seg_t")
         words = sb.tile([P, T], I32, name="words", align_bytes=64)
         scales = sb.tile([P, T], U8, name="scales", align_bytes=64)
-        w_raw = sb.tile([P, PACK, N], F32, name="w_raw", align_bytes=64)
+        w_raw = sb.tile([P, PACK, N], F32, name="w_raw", tag="staged", align_bytes=64)
         slo_t = sb.tile([P, R + SPARE], F32, name="slo_t", align_bytes=64)
         icp_t = sb.tile([P, R + SPARE], F32, name="icp_t", align_bytes=64)
         lob_t = sb.tile([P, R + SPARE], F32, name="lob_t", align_bytes=64)
@@ -69,9 +69,8 @@ def tile_picked_yrmidx_mono_p_kernel(tc, x_words, x_scales, w1, slo, icp, lob, t
         def tiles(name, dtype):
             return [sb.tile([P, HALF], dtype, name=f"{name}{h}", align_bytes=64) for h in range(2)]
 
-        lobg = tiles("lobg", F32)
-        x_codes = tiles("x_codes", U32)
-        x_bytes = tiles("x_bytes", U8)
+        x_codes = sb.tile([P, S], U32, name="x_codes", align_bytes=64)
+        x_bytes = sb.tile([P, S], U8, name="x_bytes", align_bytes=64)
         y = tiles("y", F32)
         prod = tiles("prod", F32)
         pos = tiles("pos", F32)
@@ -85,18 +84,17 @@ def tile_picked_yrmidx_mono_p_kernel(tc, x_words, x_scales, w1, slo, icp, lob, t
 
         def product(h):
             nc.tensor.matmul_mx(out=acc[h][:], lhsT=w_codes[:].bitcast(FP8X4), lhsT_scale=w_scales[:],
-                                rhs=x_codes[h][:].bitcast(FP8X4), rhs_scale=x_bytes[h][:], start=True, stop=True)
+                                rhs=x_codes[:, halves[h]].bitcast(FP8X4), rhs_scale=x_bytes[:, halves[h]], start=True, stop=True)
             nc.scalar.copy(y[h][:], acc[h][:])
 
-        for h in range(2):
-            nc.vector.tensor_copy(x_bytes[h][:], scales[:].indirect(offs_t[:, cols16[h]]))
-        for h in range(2):
-            nc.vector.tensor_copy(x_codes[h][:], words[:].bitcast(U32).indirect(offs_t[:, cols16[h]]))
+        nc.vector.tensor_copy(x_bytes[:], scales[:].indirect(offs_t[:]))
+        nc.vector.tensor_copy(x_codes[:], words[:].bitcast(U32).indirect(offs_t[:]))
         nc.vector.quantize_mx(out=w_codes[:].bitcast(FP8X4), scales=w_scales[:], in_=w_bf[:].rearrange("p n t -> p (n t)"))
         for h in range(2):
             product(h)
+        lobg = sb.tile([P, S], F32, name="lobg", tag="staged", align_bytes=64)
         for h in range(2):
-            nc.vector.tensor_copy(lobg[h][:], lob_t[:].indirect(seg_t[:, cols16[h]]))
+            nc.vector.tensor_copy(lobg[:, halves[h]], lob_t[:].indirect(seg_t[:, cols16[h]]))
         for h in range(2):
             nc.vector.tensor_tensor(prod[h][:], slo_t[:].indirect(seg_t[:, cols16[h]]), y[h][:], ALU.mult)
         for h in range(2):
@@ -104,13 +102,15 @@ def tile_picked_yrmidx_mono_p_kernel(tc, x_words, x_scales, w1, slo, icp, lob, t
         here = [slice(LEAD + h * HALF, LEAD + (h + 1) * HALF) for h in range(2)]
         before = [slice(LEAD - 1 + h * HALF, LEAD - 1 + (h + 1) * HALF) for h in range(2)]
         for h in range(2):
-            nc.vector.tensor_tensor(pcl[:, here[h]], pos[h][:], lobg[h][:], ALU.max)
+            nc.vector.tensor_tensor(pcl[:, here[h]], pos[h][:], lobg[:, halves[h]], ALU.max)
         for h in range(2):
-            nc.vector.tensor_tensor(runmax[h][:], pcl[:, before[h]], pcl[:, here[h]], ALU.max)
             nc.vector.tensor_tensor(err1[h][:], true_t[:, halves[h]], pcl[:, here[h]], ALU.subtract)
             nc.scalar.activation(sq1[h][:], err1[h][:], ACT.Square)
-            nc.vector.tensor_tensor(err2[h][:], true_t[:, halves[h]], runmax[h][:], ALU.subtract)
-            nc.scalar.activation(sq2[h][:], err2[h][:], ACT.Square)
-        for h in range(2):
-            nc.vector.scalar_tensor_tensor(res[h][:], sq2[h][:], -0.5, sq1[h][:], ALU.mult, ALU.add)
-            nc.sync.dma_start(out[:, halves[h]], res[h][:])
+            nc.vector.tensor_tensor(runmax[h][:], pcl[:, before[h]], pcl[:, here[h]], ALU.max)
+        pieces = [(0, 0, HALF), (1, 0, HALF // 2), (1, HALF // 2, HALF)]
+        for h, a, b in pieces:
+            nc.vector.tensor_tensor(err2[h][:, a:b], true_t[:, h * HALF + a : h * HALF + b], runmax[h][:, a:b], ALU.subtract)
+            nc.scalar.activation(sq2[h][:, a:b], err2[h][:, a:b], ACT.Square)
+        for h, a, b in pieces:
+            nc.vector.scalar_tensor_tensor(res[h][:, a:b], sq2[h][:, a:b], -0.5, sq1[h][:, a:b], ALU.mult, ALU.add)
+            nc.sync.dma_start(out[:, h * HALF + a : h * HALF + b], res[h][:, a:b])

@@ -80,37 +80,41 @@ def tile_picked_yrmidx_mono_p_kernel(tc, x_words, x_scales, w1, slo, icp, lob, t
         sq1 = tiles("sq1", F32)
         sq2 = tiles("sq2", F32)
         res = tiles("res", F32)
-        acc = [psum.tile([P, HALF], F32, name=f"acc{h}") for h in range(2)]
+        first = [(0, 0, HALF // 2), (0, HALF // 2, HALF), (1, 0, HALF)]
+        acc = [psum.tile([P, b - a], F32, name=f"acc{i}") for i, (h, a, b) in enumerate(first)]
 
-        def product(h):
-            nc.tensor.matmul_mx(out=acc[h][:], lhsT=w_codes[:].bitcast(FP8X4), lhsT_scale=w_scales[:],
-                                rhs=x_codes[:, halves[h]].bitcast(FP8X4), rhs_scale=x_bytes[:, halves[h]], start=True, stop=True)
-            nc.scalar.copy(y[h][:], acc[h][:])
+        def product(i):
+            h, a, b = first[i]
+            cols = slice(h * HALF + a, h * HALF + b)
+            nc.tensor.matmul_mx(out=acc[i][:], lhsT=w_codes[:].bitcast(FP8X4), lhsT_scale=w_scales[:],
+                                rhs=x_codes[:, cols].bitcast(FP8X4), rhs_scale=x_bytes[:, cols], start=True, stop=True)
+            nc.scalar.copy(y[h][:, a:b], acc[i][:])
 
         nc.vector.tensor_copy(x_bytes[:], scales[:].indirect(offs_t[:]))
         nc.vector.tensor_copy(x_codes[:], words[:].bitcast(U32).indirect(offs_t[:]))
         nc.vector.quantize_mx(out=w_codes[:].bitcast(FP8X4), scales=w_scales[:], in_=w_bf[:].rearrange("p n t -> p (n t)"))
-        for h in range(2):
-            product(h)
+        for i in range(3):
+            product(i)
         lobg = sb.tile([P, S], F32, name="lobg", tag="staged", align_bytes=64)
         for h in range(2):
             nc.vector.tensor_copy(lobg[:, halves[h]], lob_t[:].indirect(seg_t[:, cols16[h]]))
-        for h in range(2):
-            nc.vector.tensor_tensor(prod[h][:], slo_t[:].indirect(seg_t[:, cols16[h]]), y[h][:], ALU.mult)
+        for h, a, b in first:
+            nc.vector.tensor_tensor(prod[h][:, a:b], slo_t[:].indirect(seg_t[:, (h * HALF + a) // 16 : (h * HALF + b) // 16]), y[h][:, a:b], ALU.mult)
         for h in range(2):
             nc.vector.tensor_tensor(pos[h][:], icp_t[:].indirect(seg_t[:, cols16[h]]), prod[h][:], ALU.add)
         here = [slice(LEAD + h * HALF, LEAD + (h + 1) * HALF) for h in range(2)]
         before = [slice(LEAD - 1 + h * HALF, LEAD - 1 + (h + 1) * HALF) for h in range(2)]
         for h in range(2):
             nc.vector.tensor_tensor(pcl[:, here[h]], pos[h][:], lobg[:, halves[h]], ALU.max)
+        pieces = [(0, 0, HALF), (1, 0, HALF // 2), (1, HALF // 2, HALF)]
         for h in range(2):
+            nc.vector.tensor_tensor(runmax[h][:], pcl[:, before[h]], pcl[:, here[h]], ALU.max)
             nc.vector.tensor_tensor(err1[h][:], true_t[:, halves[h]], pcl[:, here[h]], ALU.subtract)
             nc.scalar.activation(sq1[h][:], err1[h][:], ACT.Square)
-            nc.vector.tensor_tensor(runmax[h][:], pcl[:, before[h]], pcl[:, here[h]], ALU.max)
-        pieces = [(0, 0, HALF), (1, 0, HALF // 2), (1, HALF // 2, HALF)]
-        for h, a, b in pieces:
-            nc.vector.tensor_tensor(err2[h][:, a:b], true_t[:, h * HALF + a : h * HALF + b], runmax[h][:, a:b], ALU.subtract)
-            nc.scalar.activation(sq2[h][:, a:b], err2[h][:, a:b], ACT.Square)
+            for hh, a, b in pieces:
+                if hh == h:
+                    nc.vector.tensor_tensor(err2[h][:, a:b], true_t[:, h * HALF + a : h * HALF + b], runmax[h][:, a:b], ALU.subtract)
+                    nc.scalar.activation(sq2[h][:, a:b], err2[h][:, a:b], ACT.Square)
         for h, a, b in pieces:
             nc.vector.scalar_tensor_tensor(res[h][:, a:b], sq2[h][:, a:b], -0.5, sq1[h][:, a:b], ALU.mult, ALU.add)
             nc.sync.dma_start(out[:, h * HALF + a : h * HALF + b], res[h][:, a:b])

@@ -36,7 +36,7 @@ def tile_picked_yrmidx_mono_p_kernel(tc, x_words, x_scales, w1, slo, icp, lob, t
         w_raw = sb.tile([P, PACK, N], F32, name="w_raw", tag="staged", align_bytes=64)
         slo_t = sb.tile([P, R + SPARE], F32, name="slo_t", align_bytes=64)
         icp_t = sb.tile([P, R + SPARE], F32, name="icp_t", align_bytes=64)
-        lob_t = sb.tile([P, R + SPARE], F32, name="lob_t", align_bytes=64)
+        lob_t = sb.tile([P, 704], F32, name="lob_t", align_bytes=64)
         true_t = sb.tile([P, S], F32, name="true_t", align_bytes=64)
         pcl = sb.tile([P, LEAD + S], F32, name="pcl", align_bytes=64)
 
@@ -59,7 +59,7 @@ def tile_picked_yrmidx_mono_p_kernel(tc, x_words, x_scales, w1, slo, icp, lob, t
         nc.sync.dma_start(true_t[:], true)
 
         w_bf = sb.tile([P, N, PACK], BF16, name="w_bf", align_bytes=64)
-        nc.scalar.activation(w_bf[:], w_raw[:].rearrange("p t n -> p n t"), ACT.Copy)
+        nc.scalar.activation(w_bf[:].rearrange("p (c i) t -> p c t i", i=4), w_raw[:].rearrange("p t (c i) -> p c t i", i=4), ACT.Copy)
         w_codes = sb.tile([P, N], U32, name="w_codes", align_bytes=64)
         w_scales = sb.tile([P, N], U8, name="w_scales", align_bytes=64)
 
@@ -96,8 +96,7 @@ def tile_picked_yrmidx_mono_p_kernel(tc, x_words, x_scales, w1, slo, icp, lob, t
         for i in range(3):
             product(i)
         lobg = sb.tile([P, S], F32, name="lobg", tag="staged", align_bytes=64)
-        for h in range(2):
-            nc.vector.tensor_copy(lobg[:, halves[h]], lob_t[:].indirect(seg_t[:, cols16[h]]))
+        nc.vector.tensor_copy(lobg[:], lob_t[:].indirect(seg_t[:]))
         for h, a, b in first:
             nc.vector.tensor_tensor(prod[h][:, a:b], slo_t[:].indirect(seg_t[:, (h * HALF + a) // 16 : (h * HALF + b) // 16]), y[h][:, a:b], ALU.mult)
         for h in range(2):

from contextlib import ExitStack

import concourse.mybir as mybir

K, T, S, N, R = 512, 1024, 512, 128, 256
FLOPS = 2 * K * N * S

F32 = mybir.dt.float32
BF16 = mybir.dt.bfloat16
I32 = mybir.dt.int32
U32 = mybir.dt.uint32
U16 = mybir.dt.uint16
U8 = mybir.dt.uint8
FP8X4 = mybir.dt.float8_e4m3fn_x4
ALU = mybir.AluOpType
ACT = mybir.ActivationFunctionType

P = 128
PACK = 4
HALF = S // 2
SPARE = 16
LEAD = 4


def tile_picked_yrmidx_mono_p_kernel(tc, x_words, x_scales, w1, slo, icp, lob, true, offs, seg, out):
    nc = tc.nc
    with ExitStack() as ctx:
        lists = ctx.enter_context(tc.tile_pool(name="lists", bufs=1))
        sb = ctx.enter_context(tc.tile_pool(name="sb", bufs=1))
        psum = ctx.enter_context(tc.psum_pool(name="psum", bufs=1))

        offs_t = lists.tile([P, S // 16], U16, name="offs_t")
        seg_t = lists.tile([P, S // 16], U16, name="seg_t")
        words = sb.tile([P, T], I32, name="words", align_bytes=64)
        scales = sb.tile([P, T], U8, name="scales", align_bytes=64)
        w_raw = sb.tile([P, PACK, N], F32, name="w_raw", tag="staged", align_bytes=64)
        slo_t = sb.tile([P, R + SPARE], F32, name="slo_t", align_bytes=64)
        icp_t = sb.tile([P, R + SPARE], F32, name="icp_t", align_bytes=64)
        lob_t = sb.tile([P, 704], F32, name="lob_t", align_bytes=64)
        true_t = sb.tile([P, S], F32, name="true_t", align_bytes=64)
        pcl = sb.tile([P, LEAD + S], F32, name="pcl", align_bytes=64)

        nc.vector.memset(lob_t[:, R:], 0.0)
        nc.vector.memset(slo_t[:, R:], 0.0)
        nc.vector.memset(icp_t[:, R:], 0.0)
        nc.vector.memset(pcl[:, 0:LEAD], 0.0)

        nc.sync.dma_start(offs_t[:], offs)
        rows = x_scales[0].bitcast(I32)
        for q in range(4):
            queue = nc.sync if q < 2 else nc.scalar
            queue.dma_start(scales[32 * q : 32 * (q + 1), :].bitcast(I32), rows[4 * q : 4 * q + 4, :].unsqueeze(0).broadcast_to([8, 4, T // 4]))
        nc.sync.dma_start(words[:], x_words[0].rearrange("p c t -> p (c t)").bitcast(I32))
        nc.sync.dma_start(w_raw[:], w1.rearrange("(p t) n -> p t n", t=PACK))
        nc.sync.dma_start(seg_t[:], seg)
        nc.sync.dma_start(lob_t[:, 0:R], lob)
        nc.sync.dma_start(slo_t[:, 0:R], slo)
        nc.sync.dma_start(icp_t[:, 0:R], icp)
        nc.sync.dma_start(true_t[:], true)

        w_bf = sb.tile([P, N, PACK], BF16, name="w_bf", align_bytes=64)
        nc.scalar.activation(w_bf[:].rearrange("p (c i) t -> p c t i", i=4), w_raw[:].rearrange("p t (c i) -> p c t i", i=4), ACT.Copy)
        w_codes = sb.tile([P, N], U32, name="w_codes", align_bytes=64)
        w_scales = sb.tile([P, N], U8, name="w_scales", align_bytes=64)

        halves = [slice(h * HALF, (h + 1) * HALF) for h in range(2)]
        cols16 = [slice(h * HALF // 16, (h + 1) * HALF // 16) for h in range(2)]

        def tiles(name, dtype):
            return [sb.tile([P, HALF], dtype, name=f"{name}{h}", align_bytes=64) for h in range(2)]

        x_codes = sb.tile([P, S], U32, name="x_codes", align_bytes=64)
        x_bytes = sb.tile([P, S], U8, name="x_bytes", align_bytes=64)
        y = tiles("y", F32)
        prod = tiles("prod", F32)
        pos = tiles("pos", F32)
        runmax = tiles("runmax", F32)
        err1 = tiles("err1", F32)
        err2 = tiles("err2", F32)
        sq1 = tiles("sq1", F32)
        sq2 = tiles("sq2", F32)
        res = tiles("res", F32)
        first = [(0, 0, HALF // 2), (0, HALF // 2, HALF), (1, 0, HALF)]
        acc = [psum.tile([P, b - a], F32, name=f"acc{i}") for i, (h, a, b) in enumerate(first)]

        def product(i):
            h, a, b = first[i]
            cols = slice(h * HALF + a, h * HALF + b)
            nc.tensor.matmul_mx(out=acc[i][:], lhsT=w_codes[:].bitcast(FP8X4), lhsT_scale=w_scales[:],
                                rhs=x_codes[:, cols].bitcast(FP8X4), rhs_scale=x_bytes[:, cols], start=True, stop=True)
            nc.scalar.copy(y[h][:, a:b], acc[i][:])

        nc.vector.tensor_copy(x_bytes[:], scales[:].indirect(offs_t[:]))
        nc.vector.tensor_copy(x_codes[:], words[:].bitcast(U32).indirect(offs_t[:]))
        nc.vector.quantize_mx(out=w_codes[:].bitcast(FP8X4), scales=w_scales[:], in_=w_bf[:].rearrange("p n t -> p (n t)"))
        for i in range(3):
            product(i)
        lobg = sb.tile([P, S], F32, name="lobg", tag="staged", align_bytes=64)
        nc.vector.tensor_copy(lobg[:], lob_t[:].indirect(seg_t[:]))
        for h, a, b in first:
            nc.vector.tensor_tensor(prod[h][:, a:b], slo_t[:].indirect(seg_t[:, (h * HALF + a) // 16 : (h * HALF + b) // 16]), y[h][:, a:b], ALU.mult)
        for h in range(2):
            nc.vector.tensor_tensor(pos[h][:], icp_t[:].indirect(seg_t[:, cols16[h]]), prod[h][:], ALU.add)
        here = [slice(LEAD + h * HALF, LEAD + (h + 1) * HALF) for h in range(2)]
        before = [slice(LEAD - 1 + h * HALF, LEAD - 1 + (h + 1) * HALF) for h in range(2)]
        for h in range(2):
            nc.vector.tensor_tensor(pcl[:, here[h]], pos[h][:], lobg[:, halves[h]], ALU.max)
        pieces = [(0, 0, HALF), (1, 0, HALF // 2), (1, HALF // 2, HALF)]
        for h in range(2):
            nc.vector.tensor_tensor(runmax[h][:], pcl[:, before[h]], pcl[:, here[h]], ALU.max)
            nc.vector.tensor_tensor(err1[h][:], true_t[:, halves[h]], pcl[:, here[h]], ALU.subtract)
            nc.scalar.activation(sq1[h][:], err1[h][:], ACT.Square)
            for hh, a, b in pieces:
                if hh == h:
                    nc.vector.tensor_tensor(err2[h][:, a:b], true_t[:, h * HALF + a : h * HALF + b], runmax[h][:, a:b], ALU.subtract)
                    nc.scalar.activation(sq2[h][:, a:b], err2[h][:, a:b], ACT.Square)
        for h, a, b in pieces:
            nc.vector.scalar_tensor_tensor(res[h][:, a:b], sq2[h][:, a:b], -0.5, sq1[h][:, a:b], ALU.mult, ALU.add)
            nc.sync.dma_start(out[:, h * HALF + a : h * HALF + b], res[h][:, a:b])
